import numpy as np
import ml_dtypes


def mxq(x, axis, fmt="e4m3"):
    dtype, down = {"e4m3": (ml_dtypes.float8_e4m3fn, 7), "e5m2": (ml_dtypes.float8_e5m2, 14)}[fmt]
    v = np.moveaxis(np.asarray(x, np.float32).astype(ml_dtypes.bfloat16).astype(np.float64), axis, -1)
    blocks = v.reshape(v.shape[:-1] + (-1, 32))
    amax = np.abs(blocks).max(-1, keepdims=True)
    byte = np.maximum(np.where(amax > 0, np.frexp(amax)[1] - 1 + 127, 0) - down, 1)
    scale = np.exp2(byte - 127.0)
    codes = (blocks / scale).astype(np.float32).astype(dtype).astype(np.float64)
    return np.moveaxis((codes * scale).reshape(v.shape), -1, axis)


WIDE = False


def mx_kscale(k):
    if not WIDE:
        return np.ones(k)
    levels = np.array([10, -10, 5, -5, 0])
    if k % 512:
        return np.exp2(np.random.permutation(np.resize(levels, k // 32))).repeat(32)
    a = np.empty((k // 512, 16))
    for p in range(k // 512):
        a[p, :8] = np.random.permutation(np.resize(levels, 8))
        for g in range(8):
            far = levels[np.abs(levels - a[p, g]) >= 10]
            a[p, g + 8] = far[np.random.randint(len(far))]
    return np.exp2(a.ravel()).repeat(32)


def f64(x):
    return np.asarray(x).astype(np.float64)


def striped8(idx):
    return np.asarray(idx).reshape(8, -1, 16).transpose(0, 2, 1).reshape(128, -1).astype(np.uint16)


def unstriped8(offs):
    return offs.reshape(8, 16, -1).transpose(0, 2, 1).reshape(8, -1).astype(np.int64)


def pick8(x, idx, run):
    r = np.arange(len(x))
    return x[r[:, None], idx[r % (8 * run) // run]]


E2M1 = np.array([0.0, 0.5, 1.0, 1.5, 2.0, 3.0, 4.0, 6.0, -0.0, -0.5, -1.0, -1.5, -2.0, -3.0, -4.0, -6.0])


def pack_weight(w, fmt):
    k, n = w.shape
    w = f64(np.asarray(w, np.float32).astype(ml_dtypes.bfloat16)).reshape(k // 32, 32, n)
    amax = np.abs(w).max(1)
    if fmt == "e4m3":
        byte = np.frexp(amax)[1] - 1 + 127 - 7
    else:
        mant, ex = np.frexp(amax / 6.0)
        byte = np.where(mant > 0.5, ex, ex - 1) + 127
    byte = np.clip(np.where(amax > 0, byte, 1), 1, 254)
    scaled = (w * np.exp2(127.0 - byte)[:, None, :]).reshape(k, n).astype(np.float32)
    by_word = np.ascontiguousarray(scaled.reshape(k // 512, 128, 4, n).transpose(0, 1, 3, 2))
    if fmt == "e4m3":
        words = by_word.astype(ml_dtypes.float8_e4m3fn).view(np.uint8)
    else:
        c = by_word.astype(ml_dtypes.float4_e2m1fn).view(np.uint8) & 0xF
        words = (c[..., 0::2] | (c[..., 1::2] << 4)).reshape(k // 512, 128, 2 * n)
    return np.ascontiguousarray(words), np.ascontiguousarray(byte.astype(np.uint8).reshape(k // 512, 16, n))


def unpack_weight(words, scales, fmt):
    g, _, n = scales.shape
    words = np.ascontiguousarray(words).reshape(g, 128, n, -1)
    if fmt == "e4m3":
        vals = words.view(ml_dtypes.float8_e4m3fn).astype(np.float64)
    else:
        nib = np.empty((g, 128, n, 4), np.uint8)
        nib[..., 0::2] = words & 0xF
        nib[..., 1::2] = words >> 4
        vals = E2M1[nib]
    vals = vals * np.repeat(np.exp2(scales.astype(np.float64) - 127.0), 8, axis=1)[..., None]
    return vals.transpose(0, 1, 3, 2).reshape(g * 512, n)


D, T, U, X, S, I, J, Q = 512, 1024, 1024, 1024, 1024, 512, 256, 128


def setup_inputs():
    n = np.random.standard_normal
    idx = np.stack([np.random.permutation(T)[:J] for _ in range(8)])
    idx2 = np.stack([np.random.permutation(U)[:J] for _ in range(8)])
    idx3 = np.stack([np.random.permutation(X)[:J] for _ in range(8)])
    idx4 = np.stack([np.random.permutation(S)[:J] for _ in range(8)])
    idx5 = np.stack([np.random.permutation(T)[:I] for _ in range(8)])
    idx6 = np.stack([np.random.permutation(T)[:I] for _ in range(8)])
    fd = mx_kscale(D)
    keysp = pack_weight(n((D, T)) / fd[:, None], "e4m3")
    notesp = pack_weight(n((D, U)) / fd[:, None], "e2m1")
    usersp = pack_weight(n((D, X)) / fd[:, None], "e4m3")
    shelvesp = pack_weight(n((D, S)) / fd[:, None], "e2m1")
    return {
        "query": (n((D, Q)) * 1.0 / np.sqrt(D) * fd[:, None]).astype(np.float32),
        "keys_words": keysp[0],
        "keys_scales": keysp[1],
        "notes_words": notesp[0],
        "notes_scales": notesp[1],
        "users_words": usersp[0],
        "users_scales": usersp[1],
        "shelves_words": shelvesp[0],
        "shelves_scales": shelvesp[1],
        "offs": striped8(idx),
        "offs2": striped8(idx2),
        "offs3": striped8(idx3),
        "offs4": striped8(idx4),
        "offs5": striped8(idx5),
        "offs6": striped8(idx6),
    }


def reference(query, keys_words, keys_scales, notes_words, notes_scales, users_words, users_scales, shelves_words, shelves_scales, offs, offs2, offs3, offs4, offs5, offs6):
    idx = unstriped8(offs)
    idx2 = unstriped8(offs2)
    idx3 = unstriped8(offs3)
    idx4 = unstriped8(offs4)
    idx5 = unstriped8(offs5)
    idx6 = unstriped8(offs6)
    keysu = unpack_weight(keys_words, keys_scales, "e4m3")
    notesu = unpack_weight(notes_words, notes_scales, "e2m1")
    usersu = unpack_weight(users_words, users_scales, "e4m3")
    shelvesu = unpack_weight(shelves_words, shelves_scales, "e2m1")
    queryq = mxq(f64(query), 0, "e4m3")
    a = queryq.T @ keysu
    b = queryq.T @ notesu
    c0 = queryq.T @ usersu
    d0 = queryq.T @ shelvesu
    w = np.concatenate([pick8(a, idx, 16), pick8(b, idx2, 16)], axis=1)
    v = np.concatenate([pick8(c0, idx3, 16), pick8(d0, idx4, 16)], axis=1)
    r = w - v
    f1 = np.zeros((Q, T))
    f1[np.arange(Q)[:, None], idx5[np.arange(Q) % 128 // 16]] = r
    aa = a + f1
    y = np.maximum(pick8(aa, idx6, 16), w)
    return y

from contextlib import ExitStack

import concourse.mybir as mybir

F32 = mybir.dt.float32
BF16 = mybir.dt.bfloat16
I32 = mybir.dt.int32
U32 = mybir.dt.uint32
U16 = mybir.dt.uint16
U8 = mybir.dt.uint8
FP8X4 = mybir.dt.float8_e4m3fn_x4
FP4X4 = mybir.dt.float4_e2m1fn_x4
ALU = mybir.AluOpType
COPY = mybir.ActivationFunctionType.Copy

P = 128
D = 512
COLS = 1024
BANK = 512
HALF = 256
FLOPS = 2 * D * P * 4 * COLS


def tile_attend_fourhalves_four_kernel(tc, query, keys_words, keys_scales, notes_words, notes_scales, users_words, users_scales, shelves_words, shelves_scales, offs, offs2, offs3, offs4, offs5, offs6, out):
    nc = tc.nc
    with ExitStack() as ctx:
        sb = ctx.enter_context(tc.tile_pool(name="sb", bufs=1))
        ps = ctx.enter_context(tc.psum_pool(name="ps", bufs=1))

        planes = {}
        for name in "nsuk":
            planes[name] = sb.tile([P, COLS], U8, name="plane_" + name, align_bytes=64)

        first = {"n": 0, "s": 0, "u": 4, "k": 8}
        scales = {"n": notes_scales, "s": shelves_scales, "u": users_scales, "k": keys_scales}

        def load_scales(name, g, eng):
            lo = 32 * g + first[name]
            eng.dma_start(out=planes[name][lo : lo + 4, :].bitcast(I32), in_=scales[name][0, 4 * g : 4 * g + 4, :].bitcast(I32))

        lists = {}

        def load_list(name, src):
            lists[name] = sb.tile(list(src.shape), U16, name=name)
            nc.sync.dma_start(lists[name][:], src)

        q_raw = sb.tile([P, 4, P], F32, name="q_raw")
        n_words = sb.tile([P, 2 * COLS], U8, name="n_words", align_bytes=64)
        s_words = sb.tile([P, 2 * COLS], U8, name="s_words", align_bytes=64)
        u_words = sb.tile([P, COLS], U32, name="u_words", align_bytes=64)
        k_words = sb.tile([P, COLS], U32, name="k_words", align_bytes=64)
        nc.sync.dma_start(out=q_raw[:], in_=query.rearrange("(p j) w -> p j w", j=4))
        load_scales("s", 0, nc.sync)
        load_scales("s", 1, nc.sync)
        load_scales("s", 2, nc.sync)
        load_scales("s", 3, nc.sync)
        nc.sync.dma_start(out=s_words[:].bitcast(I32), in_=shelves_words[0].bitcast(I32))
        nc.sync.dma_start(out=n_words[:].bitcast(I32), in_=notes_words[0].bitcast(I32))
        load_scales("n", 0, nc.sync)
        load_scales("n", 1, nc.sync)
        load_scales("n", 2, nc.sync)
        load_scales("n", 3, nc.sync)
        nc.sync.dma_start(out=u_words[:].bitcast(I32), in_=users_words[0].rearrange("p n t -> p (n t)").bitcast(I32))
        load_list("l4", offs4)
        load_list("l2", offs2)
        load_scales("u", 2, nc.sync)
        load_scales("u", 3, nc.sync)
        nc.sync.dma_start(out=k_words[:].bitcast(I32), in_=keys_words[0].rearrange("p n t -> p (n t)").bitcast(I32))
        load_list("l5", offs5)
        load_scales("k", 1, nc.sync)
        load_scales("k", 2, nc.sync)
        load_scales("k", 3, nc.sync)
        load_list("l3", offs3)
        load_list("l1", offs)
        load_list("l6", offs6)
        load_scales("u", 0, nc.gpsimd)
        load_scales("u", 1, nc.gpsimd)
        load_scales("k", 0, nc.gpsimd)

        f1 = sb.tile([P, COLS], F32, name="f1")
        nc.vector.memset(f1[:], 0.0)
        q_bf = sb.tile([P, P, 4], BF16, name="q_bf", align_bytes=64)
        nc.vector.tensor_copy(out=q_bf[:], in_=q_raw[:].rearrange("p j w -> p w j"))
        q_codes = sb.tile([P, P], U32, name="q_codes", align_bytes=64)
        q_scales = sb.tile([P, P], U8, name="q_scales", align_bytes=64)
        nc.vector.quantize_mx(out=q_codes[:].bitcast(FP8X4), scales=q_scales[:], in_=q_bf[:].rearrange("p w j -> p (w j)"))

        def scores(name, words_of, plane, first, engines):
            whole = sb.tile([P, COLS], F32, name=name)
            for h in range(2):
                bank = ps.tile([P, BANK], F32, name=name + "_ps%d" % h)
                cols = slice(h * BANK, (h + 1) * BANK)
                nc.tensor.matmul_mx(out=bank[:], lhsT=q_codes[:].bitcast(FP8X4), lhsT_scale=q_scales[:], rhs=words_of(h), rhs_scale=plane[first:P, cols], start=True, stop=True)
                if engines[h] == "v":
                    nc.vector.tensor_copy(out=whole[:, cols], in_=bank[:])
                else:
                    nc.scalar.activation(whole[:, cols], bank[:], COPY)
            return whole

        w = [sb.tile([P, HALF], F32, name="w%d" % h) for h in range(2)]
        nv = [sb.tile([P, HALF], F32, name="nv%d" % h) for h in range(2)]

        d0 = scores("d0", lambda h: s_words[:, 2 * h * BANK : 2 * (h + 1) * BANK].bitcast(FP4X4), planes["s"], 0, "sv")
        nc.scalar.activation(nv[1][:], d0[:].indirect(lists["l4"][:]), COPY, scale=-1.0)
        b = scores("b", lambda h: n_words[:, 2 * h * BANK : 2 * (h + 1) * BANK].bitcast(FP4X4), planes["n"], 0, "vv")
        nc.vector.tensor_copy(out=w[1][:], in_=b[:].indirect(lists["l2"][:]))
        nc.vector.tensor_tensor(f1[:].indirect(lists["l5"][:, 16:32]), w[1][:], nv[1][:], ALU.add)

        c0 = scores("c0", lambda h: u_words[:, h * BANK : (h + 1) * BANK].bitcast(FP8X4), planes["u"], 4, "ss")
        a = scores("a", lambda h: k_words[:, h * BANK : (h + 1) * BANK].bitcast(FP8X4), planes["k"], 8, "ss")
        nc.scalar.activation(nv[0][:], c0[:].indirect(lists["l3"][:]), COPY, scale=-1.0)
        nc.vector.tensor_copy(out=w[0][:], in_=a[:].indirect(lists["l1"][:]))
        nc.vector.tensor_tensor(f1[:].indirect(lists["l5"][:, 0:16]), w[0][:], nv[0][:], ALU.add)

        aa = sb.tile([P, COLS], F32, name="aa")
        nc.vector.tensor_tensor(aa[:], a[:], f1[:], ALU.add)
        g = [sb.tile([P, HALF], F32, name="g%d" % h) for h in range(2)]
        res = [sb.tile([P, HALF], F32, name="res%d" % h) for h in range(2)]
        nc.vector.tensor_copy(out=g[0][:], in_=aa[:].indirect(lists["l6"][:, 0:16]))
        nc.scalar.activation(g[1][:], aa[:].indirect(lists["l6"][:, 16:32]), COPY)
        for h in range(2):
            nc.vector.tensor_tensor(res[h][:], g[h][:], w[h][:], ALU.max)
            nc.sync.dma_start(out=out[:, h * HALF : (h + 1) * HALF], in_=res[h][:])
